import numpy as np
import ml_dtypes


def mxq(x, axis, fmt="e4m3"):
    dtype, down = {"e4m3": (ml_dtypes.float8_e4m3fn, 7), "e5m2": (ml_dtypes.float8_e5m2, 14)}[fmt]
    v = np.moveaxis(np.asarray(x, np.float32).astype(ml_dtypes.bfloat16).astype(np.float64), axis, -1)
    blocks = v.reshape(v.shape[:-1] + (-1, 32))
    amax = np.abs(blocks).max(-1, keepdims=True)
    byte = np.maximum(np.where(amax > 0, np.frexp(amax)[1] - 1 + 127, 0) - down, 1)
    scale = np.exp2(byte - 127.0)
    codes = (blocks / scale).astype(np.float32).astype(dtype).astype(np.float64)
    return np.moveaxis((codes * scale).reshape(v.shape), -1, axis)


WIDE = False


def mx_kscale(k):
    if not WIDE:
        return np.ones(k)
    levels = np.array([10, -10, 5, -5, 0])
    if k % 512:
        return np.exp2(np.random.permutation(np.resize(levels, k // 32))).repeat(32)
    a = np.empty((k // 512, 16))
    for p in range(k // 512):
        a[p, :8] = np.random.permutation(np.resize(levels, 8))
        for g in range(8):
            far = levels[np.abs(levels - a[p, g]) >= 10]
            a[p, g + 8] = far[np.random.randint(len(far))]
    return np.exp2(a.ravel()).repeat(32)


def f64(x):
    return np.asarray(x).astype(np.float64)


def striped(idx):
    return np.tile(idx.reshape(-1, 16).T, (8, 1)).astype(np.uint16)


def unstriped(offs):
    return offs[:16].T.reshape(-1).astype(np.int64)


def pack_weight(w):
    k, n = w.shape
    w = f64(np.asarray(w, np.float32).astype(ml_dtypes.bfloat16)).reshape(k // 32, 32, n)
    amax = np.abs(w).max(1)
    byte = np.clip(np.where(amax > 0, np.frexp(amax)[1] - 1 + 127 - 7, 1), 1, 254)
    scaled = (w * np.exp2(127.0 - byte)[:, None, :]).reshape(k, n).astype(np.float32)
    words = np.ascontiguousarray(scaled.reshape(k // 512, 128, 4, n).transpose(0, 1, 3, 2)).astype(ml_dtypes.float8_e4m3fn).view(np.uint8)
    return words, np.ascontiguousarray(byte.astype(np.uint8).reshape(k // 512, 16, n))


def unpack_weight(words, scales):
    g, p, n, _ = words.shape
    vals = np.ascontiguousarray(words).view(ml_dtypes.float8_e4m3fn).astype(np.float64) * np.repeat(np.exp2(scales.astype(np.float64) - 127.0), 8, axis=1)[..., None]
    return vals.transpose(0, 1, 3, 2).reshape(g * 512, n)


def relu(v):
    return np.maximum(v, 0.0)


K, T, S, N, U = 512, 2048, 512, 256, 1024


def setup_inputs():
    n = np.random.standard_normal
    s = mx_kscale(K)[:, None]
    packed_xT = pack_weight(n((K, T)) * s)
    return {
        "x_words": packed_xT[0],
        "x_scales": packed_xT[1],
        "w1": (n((K, N)) / np.sqrt(K) / s).astype(np.float32),
        "w2": (n((K, N)) / np.sqrt(K) / s).astype(np.float32),
        "ms": (n((N, U))).astype(np.float32),
        "hs": (np.random.uniform(0.1, 2.0, (N, U))).astype(np.float32),
        "offs": striped(np.random.permutation(T)[:S]),
        "slot": striped(np.random.permutation(U)[:S]),
    }


def reference(x_words, x_scales, w1, w2, ms, hs, offs, slot):
    msg = f64(ms)[:, unstriped(slot)]
    xq = unpack_weight(x_words, x_scales)[:, unstriped(offs)]
    yg = mxq(f64(w1), 0, "e4m3").T @ xq
    mnew = 0.8 * msg + 0.2 * yg
    hsg = f64(hs)[:, unstriped(slot)]
    yh = mxq(f64(w2), 0, "e4m3").T @ xq
    hnew = 0.9 * hsg + 0.1 * ((yh) ** 2)
    ratio = mnew / (hnew + 0.2)
    clip = ratio - relu(ratio - 1.0) + relu(-1.0 * ratio - 1.0)
    mput = mnew - (0.3 * clip)
    out = f64(ms).copy()
    out[:, unstriped(slot)] = mput
    return out

@@ -1,0 +1,176 @@
+from contextlib import ExitStack
+
+import concourse.mybir as mybir
+
+K, T, S, N, U = 512, 2048, 512, 256, 1024
+FLOPS = 2 * 2 * K * N * S
+
+F32 = mybir.dt.float32
+BF16 = mybir.dt.bfloat16
+I32 = mybir.dt.int32
+U32 = mybir.dt.uint32
+U16 = mybir.dt.uint16
+U8 = mybir.dt.uint8
+FP8X4 = mybir.dt.float8_e4m3fn_x4
+ACT = mybir.ActivationFunctionType
+ALU = mybir.AluOpType
+
+P = 128
+PACK = 4
+BLOCKS = N // P
+PIECE = 256
+PIECES = S // PIECE
+LIST_COLS = PIECE // 16
+
+
+def tile_picked_ysoph_put_p_kernel(tc, x_words, x_scales, w1, w2, ms, hs, offs, slot, out):
+    nc = tc.nc
+    with ExitStack() as ctx:
+        keep = ctx.enter_context(tc.tile_pool(name="keep", bufs=1))
+        psum = ctx.enter_context(tc.psum_pool(name="psum", bufs=1))
+
+        offs_sb = keep.tile([P, S // 16], U16, name="offs_sb")
+        slot_sb = keep.tile([P, S // 16], U16, name="slot_sb")
+        words = keep.tile([P, T], U32, name="words")
+        scales = keep.tile([P, T], U8, name="scales")
+        w_raw = [keep.tile([P, PACK, N], F32, name=f"w_raw{i}") for i in range(2)]
+        ms_sb = [keep.tile([P, U], F32, name=f"ms{b}") for b in range(BLOCKS)]
+        hs_sb = [keep.tile([P, U], F32, name=f"hs{b}") for b in range(BLOCKS)]
+
+        def rows(b):
+            return slice(b * P, (b + 1) * P)
+
+        def entries(list_tile, h):
+            return list_tile[:, h * LIST_COLS:(h + 1) * LIST_COLS]
+
+        nc.vector.memset(scales[:].bitcast(I32), 0)
+        nc.sync.dma_start(offs_sb[:], offs)
+        nc.sync.dma_start(out=words[:].bitcast(I32), in_=x_words[0].rearrange("p c r -> p (c r)").bitcast(I32))
+        for q in range(4):
+            nc.sync.dma_start(out=scales[32 * q:32 * q + 4, :].bitcast(I32), in_=x_scales[0, 4 * q:4 * q + 4, :].bitcast(I32))
+        nc.sync.dma_start(out=w_raw[1][:], in_=w2.rearrange("(p j) n -> p j n", j=PACK))
+        nc.sync.dma_start(slot_sb[:], slot)
+        nc.sync.dma_start(out=w_raw[0][:], in_=w1.rearrange("(p j) n -> p j n", j=PACK))
+        nc.sync.dma_start(out=hs_sb[0][:], in_=hs[rows(0), :])
+        nc.sync.dma_start(out=ms_sb[0][:], in_=ms[rows(0), :])
+        nc.sync.dma_start(out=hs_sb[1][:], in_=hs[rows(1), :])
+        nc.sync.dma_start(out=ms_sb[1][:], in_=ms[rows(1), :])
+
+        def interleave(i, cols, name, on_scalar):
+            width = cols.stop - cols.start
+            grouped = keep.tile([P, width, PACK], BF16, name=f"w_bf{name}", align_bytes=64)
+            dst = grouped[:].rearrange("p (c i) j -> p c j i", i=4)
+            src = w_raw[i][:, :, cols].rearrange("p j (c i) -> p c j i", i=4)
+            if on_scalar:
+                nc.scalar.copy(out=dst, in_=src)
+            else:
+                nc.vector.tensor_copy(out=dst, in_=src)
+            return grouped
+
+        def quantise(grouped, name):
+            width = grouped.shape[1]
+            codes = keep.tile([P, width], U32, name=f"w_codes{name}", align_bytes=64)
+            plane = keep.tile([P, width], U8, name=f"w_plane{name}", align_bytes=64)
+            nc.vector.quantize_mx(out=codes[:].bitcast(FP8X4), scales=plane[:], in_=grouped[:].rearrange("p n j -> p (n j)"))
+            return codes, plane
+
+        def product(codes, plane, b, h, name):
+            acc = psum.tile([P, PIECE], F32, name=f"{name}{b}{h}")
+            nc.tensor.matmul_mx(
+                out=acc[:], lhsT=codes.bitcast(FP8X4), lhsT_scale=plane,
+                rhs=x_codes[h][:].bitcast(FP8X4), rhs_scale=x_plane[h][:], start=True, stop=True,
+            )
+            return acc
+
+        def work(name, b, h, tag=None):
+            return keep.tile([P, PIECE], F32, name=f"{name}{b}{h}", tag=tag or f"{name}{b}{h}")
+
+        x_codes = []
+        for h in range(PIECES):
+            codes = keep.tile([P, PIECE], U32, name=f"x_codes{h}", align_bytes=64)
+            nc.vector.tensor_copy(codes[:], words[:].indirect(entries(offs_sb, h)))
+            x_codes.append(codes)
+        w2_bf = [interleave(1, rows(b), f"2{b}", True) for b in range(BLOCKS)]
+        x_plane = []
+        q2 = []
+        for h in range(PIECES):
+            plane = keep.tile([P, PIECE], U8, name=f"x_plane{h}", align_bytes=64)
+            nc.vector.tensor_copy(plane[:], scales[:].indirect(entries(offs_sb, h)))
+            x_plane.append(plane)
+            q2.append(quantise(w2_bf[h], f"2{h}"))
+
+        sq = {}
+        for b in range(BLOCKS):
+            for h in range(PIECES):
+                yh = product(q2[b][0][:], q2[b][1][:], b, h, "yh")
+                sq[b, h] = work("sq", b, h)
+                nc.scalar.activation(sq[b, h][:], yh[:], ACT.Square, scale=1.0 / 3.0)
+
+        def denominator(b):
+            inv = []
+            xs = []
+            for h in range(PIECES):
+                hsg = work("hsg", b, h)
+                window = hs_sb[b][:].indirect(entries(slot_sb, h))
+                if h == 0:
+                    nc.vector.tensor_copy(hsg[:], window)
+                else:
+                    nc.scalar.activation(hsg[:], window, ACT.Copy)
+                x = work("den", b, h)
+                nc.vector.scalar_tensor_tensor(x[:], sq[b, h][:], 2.0 / 9.0, hsg[:], ALU.add, ALU.add)
+                xs.append(x)
+            for h in range(PIECES):
+                root = work("root", b, h)
+                nc.scalar.activation(root[:], xs[h][:], ACT.Abs_reciprocal_sqrt, scale=1.5 if b == 0 else 3.0)
+                sgn = work("sgn", b, h)
+                if b == 0:
+                    nc.vector.tensor_scalar(sgn[:], xs[h][:], 0.0, 0.5, ALU.is_lt, ALU.subtract)
+                else:
+                    nc.scalar.activation(sgn[:], xs[h][:], ACT.Sign, scale=-1.0)
+                mag = work("mag", b, h)
+                nc.scalar.activation(mag[:], root[:], ACT.Square)
+                u = work("inv", b, h)
+                nc.vector.tensor_tensor(u[:], mag[:], sgn[:], ALU.mult)
+                inv.append(u)
+            return inv
+
+        def momentum(b, inv):
+            mnew = []
+            step = []
+            for h in range(PIECES):
+                msg = work("msg", b, h)
+                nc.scalar.activation(msg[:], ms_sb[b][:].indirect(entries(slot_sb, h)), ACT.Copy, scale=0.8)
+                m = work("mnew", b, h)
+                nc.vector.scalar_tensor_tensor(m[:], yg[b, h][:], 0.2, msg[:], ALU.mult, ALU.add)
+                mnew.append(m)
+            ratio = []
+            for h in range(PIECES):
+                r = work("ratio", b, h)
+                nc.vector.tensor_tensor(r[:], mnew[h][:], inv[h][:], ALU.mult)
+                ratio.append(r)
+            for h in range(PIECES):
+                c = work("step", b, h)
+                nc.vector.tensor_scalar(c[:], ratio[h][:], -0.3, 0.3, ALU.max, ALU.min)
+                step.append(c)
+            return mnew, step
+
+        q1 = quantise(interleave(0, slice(0, N), "1", False), "1")
+        inv0 = denominator(0)
+        yg = {}
+        for b in range(BLOCKS):
+            for h in range(PIECES):
+                yg[b, h] = product(q1[0][:, rows(b)], q1[1][:, rows(b)], b, h, "yg")
+        mnew0, step0 = momentum(0, inv0)
+        inv1 = denominator(1)
+        mput0 = []
+        for h in range(PIECES):
+            f = work("mput", 0, h, tag=f"root1{h}")
+            nc.vector.tensor_tensor(f[:], mnew0[h][:], step0[h][:], ALU.add)
+            mput0.append(f)
+        mnew1, step1 = momentum(1, inv1)
+        for h in range(PIECES):
+            nc.scalar.activation(ms_sb[0][:].indirect(entries(slot_sb, h)), mput0[h][:], ACT.Copy)
+        nc.sync.dma_start(out=out[rows(0), :], in_=ms_sb[0][:])
+        for h in range(PIECES):
+            nc.vector.tensor_tensor(ms_sb[1][:].indirect(entries(slot_sb, h)), mnew1[h][:], step1[h][:], ALU.add)
+        nc.sync.dma_start(out=out[rows(1), :], in_=ms_sb[1][:])

@@ -43,6 +43,10 @@ def tile_picked_ysoph_put_p_kernel(tc, x_words, x_scales, w1, w2, ms, hs, offs, 
         def entries(list_tile, h):
             return list_tile[:, h * LIST_COLS:(h + 1) * LIST_COLS]
 
+        warm_in = keep.tile([P, 1], F32, name="warm_in")
+        warm_out = keep.tile([P, 1], F32, name="warm_out")
+        nc.gpsimd.memset(warm_in[:], 1.0)
+        nc.scalar.activation(warm_out[:], warm_in[:], ACT.Abs_reciprocal_sqrt)
         nc.vector.memset(scales[:].bitcast(I32), 0)
         nc.sync.dma_start(offs_sb[:], offs)
         nc.sync.dma_start(out=words[:].bitcast(I32), in_=x_words[0].rearrange("p c r -> p (c r)").bitcast(I32))

@@ -49,39 +49,33 @@ def tile_picked_ysoph_put_p_kernel(tc, x_words, x_scales, w1, w2, ms, hs, offs, 
         nc.scalar.activation(warm_out[:], warm_in[:], ACT.Abs_reciprocal_sqrt)
         nc.vector.memset(scales[:].bitcast(I32), 0)
         nc.sync.dma_start(offs_sb[:], offs)
-        nc.sync.dma_start(out=words[:].bitcast(I32), in_=x_words[0].rearrange("p c r -> p (c r)").bitcast(I32))
-        for q in range(4):
-            nc.sync.dma_start(out=scales[32 * q:32 * q + 4, :].bitcast(I32), in_=x_scales[0, 4 * q:4 * q + 4, :].bitcast(I32))
         nc.sync.dma_start(out=w_raw[1][:], in_=w2.rearrange("(p j) n -> p j n", j=PACK))
         nc.sync.dma_start(slot_sb[:], slot)
-        nc.sync.dma_start(out=w_raw[0][:], in_=w1.rearrange("(p j) n -> p j n", j=PACK))
+        for q in range(4):
+            nc.sync.dma_start(out=scales[32 * q:32 * q + 4, :].bitcast(I32), in_=x_scales[0, 4 * q:4 * q + 4, :].bitcast(I32))
+        nc.sync.dma_start(out=words[:].bitcast(I32), in_=x_words[0].rearrange("p c r -> p (c r)").bitcast(I32))
         nc.sync.dma_start(out=hs_sb[0][:], in_=hs[rows(0), :])
+        nc.sync.dma_start(out=w_raw[0][:], in_=w1.rearrange("(p j) n -> p j n", j=PACK))
         nc.sync.dma_start(out=ms_sb[0][:], in_=ms[rows(0), :])
         nc.sync.dma_start(out=hs_sb[1][:], in_=hs[rows(1), :])
         nc.sync.dma_start(out=ms_sb[1][:], in_=ms[rows(1), :])
 
-        def interleave(i, cols, name, on_scalar):
-            width = cols.stop - cols.start
-            grouped = keep.tile([P, width, PACK], BF16, name=f"w_bf{name}", align_bytes=64)
-            dst = grouped[:].rearrange("p (c i) j -> p c j i", i=4)
-            src = w_raw[i][:, :, cols].rearrange("p j (c i) -> p c j i", i=4)
-            if on_scalar:
-                nc.scalar.copy(out=dst, in_=src)
-            else:
-                nc.vector.tensor_copy(out=dst, in_=src)
-            return grouped
-
-        def quantise(grouped, name):
-            width = grouped.shape[1]
-            codes = keep.tile([P, width], U32, name=f"w_codes{name}", align_bytes=64)
-            plane = keep.tile([P, width], U8, name=f"w_plane{name}", align_bytes=64)
+        def quantise(i):
+            grouped = keep.tile([P, N, PACK], BF16, name=f"w_bf{i}", align_bytes=64)
+            nc.vector.tensor_copy(
+                out=grouped[:].rearrange("p (c i) j -> p c j i", i=4),
+                in_=w_raw[i][:].rearrange("p j (c i) -> p c j i", i=4),
+            )
+            codes = keep.tile([P, N], U32, name=f"w_codes{i}", align_bytes=64)
+            plane = keep.tile([P, N], U8, name=f"w_plane{i}", align_bytes=64)
             nc.vector.quantize_mx(out=codes[:].bitcast(FP8X4), scales=plane[:], in_=grouped[:].rearrange("p n j -> p (n j)"))
             return codes, plane
 
-        def product(codes, plane, b, h, name):
+        def product(weights, b, h, name):
+            codes, plane = weights
             acc = psum.tile([P, PIECE], F32, name=f"{name}{b}{h}")
             nc.tensor.matmul_mx(
-                out=acc[:], lhsT=codes.bitcast(FP8X4), lhsT_scale=plane,
+                out=acc[:], lhsT=codes[:, rows(b)].bitcast(FP8X4), lhsT_scale=plane[:, rows(b)],
                 rhs=x_codes[h][:].bitcast(FP8X4), rhs_scale=x_plane[h][:], start=True, stop=True,
             )
             return acc
@@ -89,92 +83,94 @@ def tile_picked_ysoph_put_p_kernel(tc, x_words, x_scales, w1, w2, ms, hs, offs, 
         def work(name, b, h, tag=None):
             return keep.tile([P, PIECE], F32, name=f"{name}{b}{h}", tag=tag or f"{name}{b}{h}")
 
-        x_codes = []
-        for h in range(PIECES):
-            codes = keep.tile([P, PIECE], U32, name=f"x_codes{h}", align_bytes=64)
-            nc.vector.tensor_copy(codes[:], words[:].indirect(entries(offs_sb, h)))
-            x_codes.append(codes)
-        w2_bf = [interleave(1, rows(b), f"2{b}", True) for b in range(BLOCKS)]
+        q2 = quantise(1)
         x_plane = []
-        q2 = []
+        x_codes = []
         for h in range(PIECES):
             plane = keep.tile([P, PIECE], U8, name=f"x_plane{h}", align_bytes=64)
             nc.vector.tensor_copy(plane[:], scales[:].indirect(entries(offs_sb, h)))
             x_plane.append(plane)
-            q2.append(quantise(w2_bf[h], f"2{h}"))
+        for h in range(PIECES):
+            codes = keep.tile([P, PIECE], U32, name=f"x_codes{h}", align_bytes=64)
+            nc.vector.tensor_copy(codes[:], words[:].indirect(entries(offs_sb, h)))
+            x_codes.append(codes)
 
         sq = {}
         for b in range(BLOCKS):
             for h in range(PIECES):
-                yh = product(q2[b][0][:], q2[b][1][:], b, h, "yh")
+                yh = product(q2, b, h, "yh")
                 sq[b, h] = work("sq", b, h)
                 nc.scalar.activation(sq[b, h][:], yh[:], ACT.Square, scale=1.0 / 3.0)
 
-        def denominator(b):
-            inv = []
-            xs = []
-            for h in range(PIECES):
-                hsg = work("hsg", b, h)
-                window = hs_sb[b][:].indirect(entries(slot_sb, h))
-                if h == 0:
-                    nc.vector.tensor_copy(hsg[:], window)
-                else:
-                    nc.scalar.activation(hsg[:], window, ACT.Copy)
-                x = work("den", b, h)
-                nc.vector.scalar_tensor_tensor(x[:], sq[b, h][:], 2.0 / 9.0, hsg[:], ALU.add, ALU.add)
-                xs.append(x)
-            for h in range(PIECES):
-                root = work("root", b, h)
-                nc.scalar.activation(root[:], xs[h][:], ACT.Abs_reciprocal_sqrt, scale=1.5 if b == 0 else 3.0)
-                sgn = work("sgn", b, h)
-                if b == 0:
-                    nc.vector.tensor_scalar(sgn[:], xs[h][:], 0.0, 0.5, ALU.is_lt, ALU.subtract)
-                else:
-                    nc.scalar.activation(sgn[:], xs[h][:], ACT.Sign, scale=-1.0)
-                mag = work("mag", b, h)
-                nc.scalar.activation(mag[:], root[:], ACT.Square)
-                u = work("inv", b, h)
-                nc.vector.tensor_tensor(u[:], mag[:], sgn[:], ALU.mult)
-                inv.append(u)
-            return inv
+        den, mag, sgn, inv, msg, mnew, ratio, step, mput = {}, {}, {}, {}, {}, {}, {}, {}, {}
 
-        def momentum(b, inv):
-            mnew = []
-            step = []
-            for h in range(PIECES):
-                msg = work("msg", b, h)
-                nc.scalar.activation(msg[:], ms_sb[b][:].indirect(entries(slot_sb, h)), ACT.Copy, scale=0.8)
-                m = work("mnew", b, h)
-                nc.vector.scalar_tensor_tensor(m[:], yg[b, h][:], 0.2, msg[:], ALU.mult, ALU.add)
-                mnew.append(m)
-            ratio = []
-            for h in range(PIECES):
-                r = work("ratio", b, h)
-                nc.vector.tensor_tensor(r[:], mnew[h][:], inv[h][:], ALU.mult)
-                ratio.append(r)
-            for h in range(PIECES):
-                c = work("step", b, h)
-                nc.vector.tensor_scalar(c[:], ratio[h][:], -0.3, 0.3, ALU.max, ALU.min)
-                step.append(c)
-            return mnew, step
+        def curvature(b, h):
+            den[b, h] = work("den", b, h)
+            nc.vector.tensor_tensor(den[b, h][:], hs_sb[b][:].indirect(entries(slot_sb, h)), sq[b, h][:], ALU.add)
 
-        q1 = quantise(interleave(0, slice(0, N), "1", False), "1")
-        inv0 = denominator(0)
-        yg = {}
-        for b in range(BLOCKS):
+        def magnitude(b, h):
+            root = work("root", b, h)
+            nc.scalar.activation(root[:], den[b, h][:], ACT.Abs_reciprocal_sqrt, scale=1.5, bias=1.0 / 3.0)
+            mag[b, h] = work("mag", b, h)
+            nc.scalar.activation(mag[b, h][:], root[:], ACT.Square)
+
+        def sign(b, h):
+            sgn[b, h] = work("sgn", b, h)
+            nc.vector.tensor_scalar(sgn[b, h][:], den[b, h][:], -2.0 / 9.0, 0.5, ALU.is_lt, ALU.subtract)
+
+        def inverse(b, h):
+            inv[b, h] = work("inv", b, h)
+            nc.vector.tensor_tensor(inv[b, h][:], mag[b, h][:], sgn[b, h][:], ALU.mult)
+
+        def fetch(b, h):
+            msg[b, h] = work("msg", b, h)
+            nc.scalar.activation(msg[b, h][:], ms_sb[b][:].indirect(entries(slot_sb, h)), ACT.Copy, scale=0.8)
+
+        def momentum(b, h, tag=None):
+            mnew[b, h] = work("mnew", b, h, tag)
+            nc.vector.scalar_tensor_tensor(mnew[b, h][:], yg[b, h][:], 0.2, msg[b, h][:], ALU.mult, ALU.add)
+
+        def divide(b, h):
+            ratio[b, h] = work("ratio", b, h)
+            nc.vector.tensor_tensor(ratio[b, h][:], mnew[b, h][:], inv[b, h][:], ALU.mult)
+
+        def clip(b, h, tag=None):
+            step[b, h] = work("step", b, h, tag)
+            nc.vector.tensor_scalar(step[b, h][:], ratio[b, h][:], -0.3, 0.3, ALU.max, ALU.min)
+
+        def correct(b, h, tag=None):
+            mput[b, h] = work("mput", b, h, tag)
+            nc.vector.tensor_tensor(mput[b, h][:], mnew[b, h][:], step[b, h][:], ALU.add)
+
+        def put_scalar(b, h):
+            nc.scalar.activation(ms_sb[b][:].indirect(entries(slot_sb, h)), mput[b, h][:], ACT.Copy)
+
+        def put_vector(b, h):
+            nc.vector.tensor_tensor(ms_sb[b][:].indirect(entries(slot_sb, h)), mnew[b, h][:], step[b, h][:], ALU.add)
+
+        for h in range(PIECES):
+            curvature(0, h)
+        q1 = quantise(0)
+        yg = {(b, h): product(q1, b, h, "yg") for b in range(BLOCKS) for h in range(PIECES)}
+        for stage in (magnitude, sign, inverse, fetch):
             for h in range(PIECES):
-                yg[b, h] = product(q1[0][:, rows(b)], q1[1][:, rows(b)], b, h, "yg")
-        mnew0, step0 = momentum(0, inv0)
-        inv1 = denominator(1)
-        mput0 = []
+                stage(0, h)
         for h in range(PIECES):
-            f = work("mput", 0, h, tag=f"root1{h}")
-            nc.vector.tensor_tensor(f[:], mnew0[h][:], step0[h][:], ALU.add)
-            mput0.append(f)
-        mnew1, step1 = momentum(1, inv1)
+            curvature(1, h)
+        momentum(0, 0, tag="sq10")
+        divide(0, 0)
+        clip(0, 0)
         for h in range(PIECES):
-            nc.scalar.activation(ms_sb[0][:].indirect(entries(slot_sb, h)), mput0[h][:], ACT.Copy)
+            magnitude(1, h)
+            fetch(1, h)
+        correct(0, 0, tag="root11")
+        put_scalar(0, 0)
+        for h in range(PIECES):
+            for stage in (sign, inverse, momentum, divide, clip, correct, put_scalar):
+                stage(1, h)
+        nc.scalar.dma_start(out=out[rows(1), :], in_=ms_sb[1][:])
+        momentum(0, 1, tag="mag10")
+        divide(0, 1)
+        clip(0, 1, tag="ratio11")
+        put_vector(0, 1)
         nc.sync.dma_start(out=out[rows(0), :], in_=ms_sb[0][:])
-        for h in range(PIECES):
-            nc.vector.tensor_tensor(ms_sb[1][:].indirect(entries(slot_sb, h)), mnew1[h][:], step1[h][:], ALU.add)
-        nc.sync.dma_start(out=out[rows(1), :], in_=ms_sb[1][:])

@@ -71,106 +71,109 @@ def tile_picked_ysoph_put_p_kernel(tc, x_words, x_scales, w1, w2, ms, hs, offs, 
             nc.vector.quantize_mx(out=codes[:].bitcast(FP8X4), scales=plane[:], in_=grouped[:].rearrange("p n j -> p (n j)"))
             return codes, plane
 
-        def product(weights, b, h, name):
+        def product(weights, b, cols, name):
             codes, plane = weights
-            acc = psum.tile([P, PIECE], F32, name=f"{name}{b}{h}")
+            acc = psum.tile([P, cols.stop - cols.start], F32, name=name)
             nc.tensor.matmul_mx(
                 out=acc[:], lhsT=codes[:, rows(b)].bitcast(FP8X4), lhsT_scale=plane[:, rows(b)],
-                rhs=x_codes[h][:].bitcast(FP8X4), rhs_scale=x_plane[h][:], start=True, stop=True,
+                rhs=x_codes[:, cols].bitcast(FP8X4), rhs_scale=x_plane[:, cols], start=True, stop=True,
             )
             return acc
 
+        def piece(h):
+            return slice(h * PIECE, (h + 1) * PIECE)
+
         def work(name, b, h, tag=None):
-            return keep.tile([P, PIECE], F32, name=f"{name}{b}{h}", tag=tag or f"{name}{b}{h}")
+            return keep.tile([P, PIECE], F32, name=f"{name}{b}{h}", tag=tag or f"{name}{b}{h}")[:]
 
         q2 = quantise(1)
-        x_plane = []
-        x_codes = []
-        for h in range(PIECES):
-            plane = keep.tile([P, PIECE], U8, name=f"x_plane{h}", align_bytes=64)
-            nc.vector.tensor_copy(plane[:], scales[:].indirect(entries(offs_sb, h)))
-            x_plane.append(plane)
-        for h in range(PIECES):
-            codes = keep.tile([P, PIECE], U32, name=f"x_codes{h}", align_bytes=64)
-            nc.vector.tensor_copy(codes[:], words[:].indirect(entries(offs_sb, h)))
-            x_codes.append(codes)
+        x_plane = keep.tile([P, S], U8, name="x_plane", align_bytes=64)
+        nc.vector.tensor_copy(x_plane[:], scales[:].indirect(offs_sb[:]))
+        x_codes = keep.tile([P, S], U32, name="x_codes", align_bytes=64)
+        first_cuts = (slice(0, 128), slice(128, 256), slice(256, 512))
+        for cols in first_cuts:
+            nc.vector.tensor_copy(x_codes[:, cols], words[:].indirect(offs_sb[:, cols.start // 16:cols.stop // 16]))
 
-        sq = {}
-        for b in range(BLOCKS):
-            for h in range(PIECES):
-                yh = product(q2, b, h, "yh")
-                sq[b, h] = work("sq", b, h)
-                nc.scalar.activation(sq[b, h][:], yh[:], ACT.Square, scale=1.0 / 3.0)
+        sq = {(b, h): work("sq", b, h) for b in range(BLOCKS) for h in range(PIECES)}
+        for cols in first_cuts:
+            yh = product(q2, 0, cols, f"yh0_{cols.start}")
+            h, lo = divmod(cols.start, PIECE)
+            nc.scalar.activation(sq[0, h][:, lo:lo + cols.stop - cols.start], yh[:], ACT.Square, scale=1.0 / 3.0)
+        for h in range(PIECES):
+            yh = product(q2, 1, piece(h), f"yh1_{h}")
+            nc.scalar.activation(sq[1, h], yh[:], ACT.Square, scale=1.0 / 3.0)
 
         den, mag, sgn, inv, msg, mnew, ratio, step, mput = {}, {}, {}, {}, {}, {}, {}, {}, {}
+        mnew1 = keep.tile([P, S], F32, name="mnew1")
+        step1 = keep.tile([P, S], F32, name="step1")
 
         def curvature(b, h):
             den[b, h] = work("den", b, h)
-            nc.vector.tensor_tensor(den[b, h][:], hs_sb[b][:].indirect(entries(slot_sb, h)), sq[b, h][:], ALU.add)
+            nc.vector.tensor_tensor(den[b, h], hs_sb[b][:].indirect(entries(slot_sb, h)), sq[b, h], ALU.add)
 
         def magnitude(b, h):
             root = work("root", b, h)
-            nc.scalar.activation(root[:], den[b, h][:], ACT.Abs_reciprocal_sqrt, scale=1.5, bias=1.0 / 3.0)
-            mag[b, h] = work("mag", b, h)
-            nc.scalar.activation(mag[b, h][:], root[:], ACT.Square)
-
-        def sign(b, h):
+            nc.scalar.activation(root, den[b, h], ACT.Abs_reciprocal_sqrt, scale=3.0, bias=2.0 / 3.0)
             sgn[b, h] = work("sgn", b, h)
-            nc.vector.tensor_scalar(sgn[b, h][:], den[b, h][:], -2.0 / 9.0, 0.5, ALU.is_lt, ALU.subtract)
+            nc.scalar.activation(sgn[b, h], den[b, h], ACT.Sign, scale=-3.0, bias=-2.0 / 3.0)
+            mag[b, h] = work("mag", b, h)
+            nc.scalar.activation(mag[b, h], root, ACT.Square)
 
-        def inverse(b, h):
-            inv[b, h] = work("inv", b, h)
-            nc.vector.tensor_tensor(inv[b, h][:], mag[b, h][:], sgn[b, h][:], ALU.mult)
+        def inverse(b, h, tag=None):
+            inv[b, h] = work("inv", b, h, tag)
+            nc.vector.tensor_tensor(inv[b, h], mag[b, h], sgn[b, h], ALU.mult)
 
         def fetch(b, h):
             msg[b, h] = work("msg", b, h)
-            nc.scalar.activation(msg[b, h][:], ms_sb[b][:].indirect(entries(slot_sb, h)), ACT.Copy, scale=0.8)
+            nc.scalar.activation(msg[b, h], ms_sb[b][:].indirect(entries(slot_sb, h)), ACT.Copy, scale=0.8)
 
-        def momentum(b, h, tag=None):
-            mnew[b, h] = work("mnew", b, h, tag)
-            nc.vector.scalar_tensor_tensor(mnew[b, h][:], yg[b, h][:], 0.2, msg[b, h][:], ALU.mult, ALU.add)
+        def momentum(b, h, dst):
+            mnew[b, h] = dst
+            nc.vector.scalar_tensor_tensor(dst, yg[b][:, piece(h)], 0.2, msg[b, h], ALU.mult, ALU.add)
 
         def divide(b, h):
             ratio[b, h] = work("ratio", b, h)
-            nc.vector.tensor_tensor(ratio[b, h][:], mnew[b, h][:], inv[b, h][:], ALU.mult)
+            nc.vector.tensor_tensor(ratio[b, h], mnew[b, h], inv[b, h], ALU.mult)
 
-        def clip(b, h, tag=None):
-            step[b, h] = work("step", b, h, tag)
-            nc.vector.tensor_scalar(step[b, h][:], ratio[b, h][:], -0.3, 0.3, ALU.max, ALU.min)
+        def clip(b, h, dst):
+            step[b, h] = dst
+            nc.vector.tensor_scalar(dst, ratio[b, h], -0.3, 0.3, ALU.max, ALU.min)
 
-        def correct(b, h, tag=None):
+        def correct(b, h, tag):
             mput[b, h] = work("mput", b, h, tag)
-            nc.vector.tensor_tensor(mput[b, h][:], mnew[b, h][:], step[b, h][:], ALU.add)
+            nc.vector.tensor_tensor(mput[b, h], mnew[b, h], step[b, h], ALU.add)
 
-        def put_scalar(b, h):
-            nc.scalar.activation(ms_sb[b][:].indirect(entries(slot_sb, h)), mput[b, h][:], ACT.Copy)
-
-        def put_vector(b, h):
-            nc.vector.tensor_tensor(ms_sb[b][:].indirect(entries(slot_sb, h)), mnew[b, h][:], step[b, h][:], ALU.add)
-
-        for h in range(PIECES):
+        both = range(PIECES)
+        for h in both:
             curvature(0, h)
         q1 = quantise(0)
-        yg = {(b, h): product(q1, b, h, "yg") for b in range(BLOCKS) for h in range(PIECES)}
-        for stage in (magnitude, sign, inverse, fetch):
-            for h in range(PIECES):
+        yg = [product(q1, b, slice(0, S), f"yg{b}") for b in range(BLOCKS)]
+        for stage in (magnitude, inverse, fetch):
+            for h in both:
                 stage(0, h)
-        for h in range(PIECES):
+        for h in both:
             curvature(1, h)
-        momentum(0, 0, tag="sq10")
-        divide(0, 0)
-        clip(0, 0)
-        for h in range(PIECES):
-            magnitude(1, h)
-            fetch(1, h)
-        correct(0, 0, tag="root11")
-        put_scalar(0, 0)
-        for h in range(PIECES):
-            for stage in (sign, inverse, momentum, divide, clip, correct, put_scalar):
+        for h in both:
+            momentum(0, h, work("mnew", 0, h, tag=f"sq1{h}"))
+        for h in both:
+            divide(0, h)
+        for h in both:
+            clip(0, h, work("step", 0, h))
+        for stage in (magnitude, fetch):
+            for h in both:
                 stage(1, h)
-        nc.scalar.dma_start(out=out[rows(1), :], in_=ms_sb[1][:])
-        momentum(0, 1, tag="mag10")
-        divide(0, 1)
-        clip(0, 1, tag="ratio11")
-        put_vector(0, 1)
-        nc.sync.dma_start(out=out[rows(0), :], in_=ms_sb[0][:])
+        correct(0, 0, tag="root10")
+        correct(0, 1, tag=None)
+        for h in both:
+            nc.scalar.activation(ms_sb[0][:].indirect(entries(slot_sb, h)), mput[0, h], ACT.Copy)
+        nc.scalar.dma_start(out=out[rows(0), :], in_=ms_sb[0][:])
+        inverse(1, 0, tag="ratio00")
+        inverse(1, 1)
+        for h in both:
+            momentum(1, h, mnew1[:, piece(h)])
+        for h in both:
+            divide(1, h)
+        for h in both:
+            clip(1, h, step1[:, piece(h)])
+        nc.vector.tensor_tensor(ms_sb[1][:].indirect(slot_sb[:]), mnew1[:], step1[:], ALU.add)
+        nc.sync.dma_start(out=out[rows(1), :], in_=ms_sb[1][:])

from contextlib import ExitStack

import concourse.mybir as mybir

K, T, S, N, U = 512, 2048, 512, 256, 1024
FLOPS = 2 * 2 * K * N * S

F32 = mybir.dt.float32
BF16 = mybir.dt.bfloat16
I32 = mybir.dt.int32
U32 = mybir.dt.uint32
U16 = mybir.dt.uint16
U8 = mybir.dt.uint8
FP8X4 = mybir.dt.float8_e4m3fn_x4
ACT = mybir.ActivationFunctionType
ALU = mybir.AluOpType

P = 128
PACK = 4
BLOCKS = N // P
PIECE = 256
PIECES = S // PIECE
LIST_COLS = PIECE // 16


def tile_picked_ysoph_put_p_kernel(tc, x_words, x_scales, w1, w2, ms, hs, offs, slot, out):
    nc = tc.nc
    with ExitStack() as ctx:
        keep = ctx.enter_context(tc.tile_pool(name="keep", bufs=1))
        psum = ctx.enter_context(tc.psum_pool(name="psum", bufs=1))

        offs_sb = keep.tile([P, S // 16], U16, name="offs_sb")
        slot_sb = keep.tile([P, S // 16], U16, name="slot_sb")
        words = keep.tile([P, T], U32, name="words")
        scales = keep.tile([P, T], U8, name="scales")
        w_raw = [keep.tile([P, PACK, N], F32, name=f"w_raw{i}") for i in range(2)]
        ms_sb = [keep.tile([P, U], F32, name=f"ms{b}") for b in range(BLOCKS)]
        hs_sb = [keep.tile([P, U], F32, name=f"hs{b}") for b in range(BLOCKS)]

        def rows(b):
            return slice(b * P, (b + 1) * P)

        def entries(list_tile, h):
            return list_tile[:, h * LIST_COLS:(h + 1) * LIST_COLS]

        warm_in = keep.tile([P, 1], F32, name="warm_in")
        warm_out = keep.tile([P, 1], F32, name="warm_out")
        nc.gpsimd.memset(warm_in[:], 1.0)
        nc.scalar.activation(warm_out[:], warm_in[:], ACT.Abs_reciprocal_sqrt)
        nc.vector.memset(scales[:].bitcast(I32), 0)
        nc.sync.dma_start(offs_sb[:], offs)
        nc.sync.dma_start(out=w_raw[1][:], in_=w2.rearrange("(p j) n -> p j n", j=PACK))
        nc.sync.dma_start(slot_sb[:], slot)
        for q in range(4):
            nc.sync.dma_start(out=scales[32 * q:32 * q + 4, :].bitcast(I32), in_=x_scales[0, 4 * q:4 * q + 4, :].bitcast(I32))
        nc.sync.dma_start(out=words[:].bitcast(I32), in_=x_words[0].rearrange("p c r -> p (c r)").bitcast(I32))
        nc.sync.dma_start(out=hs_sb[0][:], in_=hs[rows(0), :])
        nc.sync.dma_start(out=w_raw[0][:], in_=w1.rearrange("(p j) n -> p j n", j=PACK))
        nc.sync.dma_start(out=ms_sb[0][:], in_=ms[rows(0), :])
        nc.sync.dma_start(out=hs_sb[1][:], in_=hs[rows(1), :])
        nc.sync.dma_start(out=ms_sb[1][:], in_=ms[rows(1), :])

        def quantise(i):
            grouped = keep.tile([P, N, PACK], BF16, name=f"w_bf{i}", align_bytes=64)
            nc.vector.tensor_copy(
                out=grouped[:].rearrange("p (c i) j -> p c j i", i=4),
                in_=w_raw[i][:].rearrange("p j (c i) -> p c j i", i=4),
            )
            codes = keep.tile([P, N], U32, name=f"w_codes{i}", align_bytes=64)
            plane = keep.tile([P, N], U8, name=f"w_plane{i}", align_bytes=64)
            nc.vector.quantize_mx(out=codes[:].bitcast(FP8X4), scales=plane[:], in_=grouped[:].rearrange("p n j -> p (n j)"))
            return codes, plane

        def product(weights, b, cols, name):
            codes, plane = weights
            acc = psum.tile([P, cols.stop - cols.start], F32, name=name)
            nc.tensor.matmul_mx(
                out=acc[:], lhsT=codes[:, rows(b)].bitcast(FP8X4), lhsT_scale=plane[:, rows(b)],
                rhs=x_codes[:, cols].bitcast(FP8X4), rhs_scale=x_plane[:, cols], start=True, stop=True,
            )
            return acc

        def piece(h):
            return slice(h * PIECE, (h + 1) * PIECE)

        def work(name, b, h, tag=None):
            return keep.tile([P, PIECE], F32, name=f"{name}{b}{h}", tag=tag or f"{name}{b}{h}")[:]

        q2 = quantise(1)
        x_plane = keep.tile([P, S], U8, name="x_plane", align_bytes=64)
        nc.vector.tensor_copy(x_plane[:], scales[:].indirect(offs_sb[:]))
        x_codes = keep.tile([P, S], U32, name="x_codes", align_bytes=64)
        first_cuts = (slice(0, 128), slice(128, 256), slice(256, 512))
        for cols in first_cuts:
            nc.vector.tensor_copy(x_codes[:, cols], words[:].indirect(offs_sb[:, cols.start // 16:cols.stop // 16]))

        sq = {(b, h): work("sq", b, h) for b in range(BLOCKS) for h in range(PIECES)}
        for cols in first_cuts:
            yh = product(q2, 0, cols, f"yh0_{cols.start}")
            h, lo = divmod(cols.start, PIECE)
            nc.scalar.activation(sq[0, h][:, lo:lo + cols.stop - cols.start], yh[:], ACT.Square, scale=1.0 / 3.0)
        for h in range(PIECES):
            yh = product(q2, 1, piece(h), f"yh1_{h}")
            nc.scalar.activation(sq[1, h], yh[:], ACT.Square, scale=1.0 / 3.0)

        den, mag, sgn, inv, msg, mnew, ratio, step, mput = {}, {}, {}, {}, {}, {}, {}, {}, {}
        mnew1 = keep.tile([P, S], F32, name="mnew1")
        step1 = keep.tile([P, S], F32, name="step1")

        def curvature(b, h):
            den[b, h] = work("den", b, h)
            nc.vector.tensor_tensor(den[b, h], hs_sb[b][:].indirect(entries(slot_sb, h)), sq[b, h], ALU.add)

        def magnitude(b, h):
            root = work("root", b, h)
            nc.scalar.activation(root, den[b, h], ACT.Abs_reciprocal_sqrt, scale=3.0, bias=2.0 / 3.0)
            sgn[b, h] = work("sgn", b, h)
            nc.scalar.activation(sgn[b, h], den[b, h], ACT.Sign, scale=-3.0, bias=-2.0 / 3.0)
            mag[b, h] = work("mag", b, h)
            nc.scalar.activation(mag[b, h], root, ACT.Square)

        def inverse(b, h, tag=None):
            inv[b, h] = work("inv", b, h, tag)
            nc.vector.tensor_tensor(inv[b, h], mag[b, h], sgn[b, h], ALU.mult)

        def fetch(b, h):
            msg[b, h] = work("msg", b, h)
            nc.scalar.activation(msg[b, h], ms_sb[b][:].indirect(entries(slot_sb, h)), ACT.Copy, scale=0.8)

        def momentum(b, h, dst):
            mnew[b, h] = dst
            nc.vector.scalar_tensor_tensor(dst, yg[b][:, piece(h)], 0.2, msg[b, h], ALU.mult, ALU.add)

        def divide(b, h):
            ratio[b, h] = work("ratio", b, h)
            nc.vector.tensor_tensor(ratio[b, h], mnew[b, h], inv[b, h], ALU.mult)

        def clip(b, h, dst):
            step[b, h] = dst
            nc.vector.tensor_scalar(dst, ratio[b, h], -0.3, 0.3, ALU.max, ALU.min)

        def correct(b, h, tag):
            mput[b, h] = work("mput", b, h, tag)
            nc.vector.tensor_tensor(mput[b, h], mnew[b, h], step[b, h], ALU.add)

        both = range(PIECES)
        for h in both:
            curvature(0, h)
        q1 = quantise(0)
        yg = [product(q1, b, slice(0, S), f"yg{b}") for b in range(BLOCKS)]
        for stage in (magnitude, inverse, fetch):
            for h in both:
                stage(0, h)
        for h in both:
            curvature(1, h)
        for h in both:
            momentum(0, h, work("mnew", 0, h, tag=f"sq1{h}"))
        for h in both:
            divide(0, h)
        for h in both:
            clip(0, h, work("step", 0, h))
        for stage in (magnitude, fetch):
            for h in both:
                stage(1, h)
        correct(0, 0, tag="root10")
        correct(0, 1, tag=None)
        for h in both:
            nc.scalar.activation(ms_sb[0][:].indirect(entries(slot_sb, h)), mput[0, h], ACT.Copy)
        nc.scalar.dma_start(out=out[rows(0), :], in_=ms_sb[0][:])
        inverse(1, 0, tag="ratio00")
        inverse(1, 1)
        for h in both:
            momentum(1, h, mnew1[:, piece(h)])
        for h in both:
            divide(1, h)
        for h in both:
            clip(1, h, step1[:, piece(h)])
        nc.vector.tensor_tensor(ms_sb[1][:].indirect(slot_sb[:]), mnew1[:], step1[:], ALU.add)
        nc.sync.dma_start(out=out[rows(1), :], in_=ms_sb[1][:])
